import numpy as np
import ml_dtypes


def mxq(x, axis, fmt="e4m3"):
    dtype, down = {"e4m3": (ml_dtypes.float8_e4m3fn, 7), "e5m2": (ml_dtypes.float8_e5m2, 14)}[fmt]
    v = np.moveaxis(np.asarray(x, np.float32).astype(ml_dtypes.bfloat16).astype(np.float64), axis, -1)
    blocks = v.reshape(v.shape[:-1] + (-1, 32))
    amax = np.abs(blocks).max(-1, keepdims=True)
    byte = np.maximum(np.where(amax > 0, np.frexp(amax)[1] - 1 + 127, 0) - down, 1)
    scale = np.exp2(byte - 127.0)
    codes = (blocks / scale).astype(np.float32).astype(dtype).astype(np.float64)
    return np.moveaxis((codes * scale).reshape(v.shape), -1, axis)


WIDE = False


def mx_kscale(k):
    if not WIDE:
        return np.ones(k)
    levels = np.array([10, -10, 5, -5, 0])
    if k % 512:
        return np.exp2(np.random.permutation(np.resize(levels, k // 32))).repeat(32)
    a = np.empty((k // 512, 16))
    for p in range(k // 512):
        a[p, :8] = np.random.permutation(np.resize(levels, 8))
        for g in range(8):
            far = levels[np.abs(levels - a[p, g]) >= 10]
            a[p, g + 8] = far[np.random.randint(len(far))]
    return np.exp2(a.ravel()).repeat(32)


def f64(x):
    return np.asarray(x).astype(np.float64)


def striped(idx):
    return np.tile(np.asarray(idx).reshape(-1, 16).T, (8, 1)).astype(np.uint16)


def unstriped(offs):
    return offs[:16].T.reshape(-1).astype(np.int64)


def bf(x):
    return np.asarray(x, np.float32).astype(ml_dtypes.bfloat16)


def planes(Y):
    r, m = Y.shape
    b = f64(bf(Y)).reshape(r // 32, 32, m)
    amax = np.abs(b).max(1)
    byte = np.clip(np.where(amax > 0, np.frexp(amax)[1] - 1 + 127 - 7, 1), 1, 254)
    codes = (b * np.exp2(127.0 - byte)[:, None, :]).reshape(r, m).astype(np.float32).astype(ml_dtypes.float8_e4m3fn).view(np.uint8)
    words = codes.reshape(r // 512, 128, 4, m).transpose(0, 1, 3, 2)
    return np.ascontiguousarray(words), np.ascontiguousarray(byte.astype(np.uint8).reshape(r // 512, 16, m))


D, T, I, Q = 512, 2048, 512, 512


def setup_inputs():
    n = np.random.standard_normal
    idx = np.random.permutation(T)[:I]
    fd = mx_kscale(D)
    return {
        "query": (n((D, Q)) * 0.8 / np.sqrt(D) * fd[:, None]).astype(np.float32),
        "keys": (n((D, T)) * np.random.uniform(0.4, 2.0, (1, T))).astype(np.float32),
        "dsc": (np.random.uniform(0.5, 2.0, (1, D)) / fd).astype(np.float32),
        "lim": (np.random.uniform(0.6, 1.2, (I, 1))).astype(np.float32),
        "offs": striped(idx),
    }


def reference(query, keys, dsc, lim, offs):
    idx = unstriped(offs)
    kt = f64(keys)[:, idx].T
    nr = np.sqrt(np.mean(np.square(kt), axis=1, keepdims=True))
    ks = kt * np.minimum(f64(lim) / nr, 1.0) * f64(dsc)
    km = ks.T
    queryq = mxq(f64(query), 0, "e4m3")
    kmq = mxq(km, 0, "e4m3")
    a = queryq.T @ kmq
    p = np.exp(a - np.max(a, axis=1, keepdims=True))
    y = p / np.sum(p, axis=1, keepdims=True) * 512.0
    words, scales = planes(y)
    return y, words, scales

@@ -1,0 +1,226 @@
+from contextlib import ExitStack
+
+import concourse.mybir as mybir
+from concourse.masks import make_identity
+
+D, T, I, Q = 512, 2048, 512, 512
+FLOPS = 2 * D * I * Q
+
+F32 = mybir.dt.float32
+BF16 = mybir.dt.bfloat16
+I32 = mybir.dt.int32
+U32 = mybir.dt.uint32
+U16 = mybir.dt.uint16
+U8 = mybir.dt.uint8
+FP8X4 = mybir.dt.float8_e4m3fn_x4
+ALU = mybir.AluOpType
+ACT = mybir.ActivationFunctionType
+AX = mybir.AxisListType
+
+P = 128
+PACK = 4
+HALF = I // 2
+SPLIT = 320
+
+
+def tile_attend_clippedkeys_pl_kernel(tc, query, keys, dsc, lim, offs, out_0, out_1, out_2):
+    nc = tc.nc
+    with ExitStack() as ctx:
+        sb = ctx.enter_context(tc.tile_pool(name="sb", bufs=1))
+        ps = ctx.enter_context(tc.psum_pool(name="ps", bufs=1))
+
+        offsets = sb.tile([P, I // 16], U16, name="offsets")
+        pool_planes = [sb.tile([P, T], F32, name="pool%d" % t) for t in range(PACK)]
+        q_raw = sb.tile([P, PACK, Q], F32, name="q_raw")
+        key_rows = keys.rearrange("(p t) n -> p t n", t=PACK)
+        nc.sync.dma_start(pool_planes[0][:], key_rows[:, 0, :])
+        nc.sync.dma_start(offsets[:], offs)
+        dsc_cols = sb.tile([P, PACK], F32, name="dsc_cols")
+        nc.sync.dma_start(dsc_cols[:], dsc.rearrange("o (p t) -> p (o t)", t=PACK))
+        lim_rows = sb.tile([P, P], F32, name="lim_rows")
+        nc.gpsimd.memset(lim_rows[:], 0.0)
+        nc.sync.dma_start(lim_rows[0:4, :], lim.rearrange("(j p) o -> j (p o)", p=P))
+        for t in range(1, PACK):
+            nc.sync.dma_start(pool_planes[t][:], key_rows[:, t, :])
+        nc.sync.dma_start(q_raw[:], query.rearrange("(p t) n -> p t n", t=PACK))
+
+        warm_in = sb.tile([P, 1], F32, name="warm_in")
+        warm_out = sb.tile([P, 1], F32, name="warm_out")
+        nc.vector.memset(warm_in[:], 1.0)
+        nc.scalar.activation(warm_out[:], warm_in[:], ACT.Sqrt)
+
+        ident = sb.tile([P, P], F32, name="ident")
+        make_identity(nc, ident[:])
+        lim_ps = ps.tile([P, I], F32, name="lim_ps", tag="turn", bufs=2)
+        nc.tensor.transpose(lim_ps[:, 0:P], lim_rows[:], ident[:])
+        lim_cols = sb.tile([P, 4], F32, name="lim_cols")
+        nc.scalar.copy(lim_cols[:], lim_ps[:, 0:4])
+
+        squares = sb.tile([P, PACK, I], BF16, name="squares")
+        mean_sq = sb.tile([P, PACK, 4], F32, name="mean_sq")
+        scaled = [sb.tile([P, PACK, HALF], F32, name="scaled%d" % h) for h in range(2)]
+
+        def square_blocks(t, picked, first_block, n_blocks):
+            turned = ps.tile([P, I], F32, name="turned", tag="turn", bufs=2)
+            for b in range(n_blocks):
+                nc.tensor.transpose(turned[:, b * P : (b + 1) * P], picked[:, b * P : (b + 1) * P], ident[:])
+            for b in range(n_blocks):
+                j = first_block + b
+                nc.scalar.activation(
+                    squares[:, t, j * P : (j + 1) * P],
+                    turned[:, b * P : (b + 1) * P],
+                    ACT.Square,
+                    scale=D**-0.5,
+                    accum_out=mean_sq[:, t, j : j + 1],
+                )
+
+        def scale_features(t, h, picked):
+            nc.vector.tensor_scalar(scaled[h][:, t, :], picked, dsc_cols[:, t : t + 1], None, ALU.mult)
+
+        for t in range(PACK - 1):
+            picked = sb.tile([P, I], F32, name="picked%d" % t)
+            nc.vector.tensor_copy(picked[:], pool_planes[t][:].indirect(offsets[:]))
+            square_blocks(t, picked, 0, 4)
+            for h in range(2):
+                scale_features(t, h, picked[:, h * HALF : (h + 1) * HALF])
+        sum01 = sb.tile([P, 4], F32, name="sum01")
+        sum012 = sb.tile([P, 4], F32, name="sum012")
+        nc.gpsimd.tensor_tensor(sum01[:], mean_sq[:, 0, :], mean_sq[:, 1, :], ALU.add)
+        nc.gpsimd.tensor_tensor(sum012[:], sum01[:], mean_sq[:, 2, :], ALU.add)
+
+        last = PACK - 1
+        picked_last = [sb.tile([P, HALF], F32, name="picked_last%d" % h) for h in range(2)]
+        rms = sb.tile([P, 4], F32, name="rms")
+        inv_rms = sb.tile([P, 4], F32, name="inv_rms")
+        for h in range(2):
+            nc.vector.tensor_copy(picked_last[h][:], pool_planes[last][:].indirect(offsets[:, 16 * h : 16 * (h + 1)]))
+            square_blocks(last, picked_last[h], 2 * h, 2)
+            for j in (2 * h, 2 * h + 1):
+                nc.scalar.activation(
+                    rms[:, j : j + 1],
+                    mean_sq[:, last, j : j + 1],
+                    ACT.Sqrt,
+                    bias=sum012[:, j : j + 1],
+                )
+        for h in range(2):
+            scale_features(last, h, picked_last[h][:])
+
+        shrink = sb.tile([P, 4], F32, name="shrink")
+        spread = []
+        for h in range(2):
+            bank = ps.tile([P, I], F32, name="spread%d" % h)
+            nc.vector.reciprocal(inv_rms[:, 2 * h : 2 * h + 2], rms[:, 2 * h : 2 * h + 2])
+            for b in range(2):
+                j = 2 * h + b
+                nc.vector.tensor_scalar(
+                    shrink[:, j : j + 1], inv_rms[:, j : j + 1], lim_cols[:, j : j + 1], 1.0, ALU.mult, ALU.min
+                )
+            for b in range(2):
+                j = 2 * h + b
+                nc.tensor.transpose(bank[:, b * P : (b + 1) * P], shrink[:, j : j + 1].to_broadcast([P, P]), ident[:])
+            spread.append(bank)
+
+        q_bf = [sb.tile([P, 2, P, PACK], BF16, name="q_bf%d" % u, align_bytes=64) for u in range(2)]
+        q_codes = [sb.tile([P, 2 * P], U32, name="q_codes%d" % u, align_bytes=64) for u in range(2)]
+        q_scales = [sb.tile([P, 2 * P], U8, name="q_scales%d" % u, align_bytes=64) for u in range(2)]
+        q_dealt = q_raw[:].rearrange("p t (m u e) -> p u m t e", u=2, e=2)
+        for u in range(2):
+            nc.scalar.copy(q_bf[u][:].rearrange("p e m t -> p m t e"), q_dealt[:, u])
+
+        k_bf = [sb.tile([P, HALF, PACK], BF16, name="k_bf%d" % h, align_bytes=64) for h in range(2)]
+        k_codes = [sb.tile([P, HALF], U32, name="k_codes%d" % h, align_bytes=64) for h in range(2)]
+        k_scales = [sb.tile([P, HALF], U8, name="k_scales%d" % h, align_bytes=64) for h in range(2)]
+
+        def shrink_keys(h):
+            nc.vector.tensor_tensor(
+                k_bf[h][:].rearrange("p (c i) t -> p c t i", i=4),
+                scaled[h][:].rearrange("p t (c i) -> p c t i", i=4),
+                spread[h][:, 0:HALF].rearrange("p (c i) -> p c i", i=4).unsqueeze(2).to_broadcast([P, HALF // 4, PACK, 4]),
+                ALU.mult,
+            )
+
+        def quantize(codes, scales, values):
+            nc.vector.quantize_mx(out=codes.bitcast(FP8X4), scales=scales, in_=values)
+
+        scores = [ps.tile([P, I], F32, name="scores%d" % r) for r in range(PACK)]
+
+        def score(r, h):
+            u, e = divmod(r, 2)
+            nc.tensor.matmul_mx(
+                out=scores[r][:, h * HALF : (h + 1) * HALF],
+                lhsT=q_codes[u][:, e * P : (e + 1) * P].bitcast(FP8X4),
+                lhsT_scale=q_scales[u][:, e * P : (e + 1) * P],
+                rhs=k_codes[h][:].bitcast(FP8X4),
+                rhs_scale=k_scales[h][:],
+                start=True,
+                stop=True,
+            )
+
+        def quantize_keys(h):
+            quantize(k_codes[h][:], k_scales[h][:], k_bf[h][:].rearrange("p i t -> p (i t)"))
+
+        def quantize_queries(u):
+            quantize(q_codes[u][:], q_scales[u][:], q_bf[u][:].rearrange("p e m t -> p (e m t)"))
+
+        shrink_keys(0)
+        shrink_keys(1)
+        quantize_keys(0)
+        quantize_queries(0)
+        score(0, 0)
+        score(1, 0)
+        quantize_keys(1)
+        score(0, 1)
+        score(1, 1)
+        quantize_queries(1)
+        for r in (2, 3):
+            for h in range(2):
+                score(r, h)
+
+        neg_max = sb.tile([P, PACK], F32, name="neg_max")
+        row_sum = sb.tile([P, PACK], F32, name="row_sum")
+        inv_sum = sb.tile([P, PACK], F32, name="inv_sum")
+        weights = [sb.tile([P, I], F32, name="weights%d" % r) for r in range(PACK)]
+        y = sb.tile([P, PACK, I], F32, name="y")
+        out_rows = out_0.rearrange("(p r) i -> p r i", r=PACK)
+
+        def row_max(r):
+            nc.vector.tensor_reduce(neg_max[:, r : r + 1], scores[r][:], AX.X, ALU.max, negate=True)
+
+        def exponentiate(r):
+            nc.scalar.activation(
+                weights[r][:], scores[r][:], ACT.Exp, bias=neg_max[:, r : r + 1], accum_out=row_sum[:, r : r + 1]
+            )
+
+        def normalise(r, engine):
+            nc.vector.reciprocal(inv_sum[:, r : r + 1], row_sum[:, r : r + 1])
+            engine.tensor_scalar(y[:, r, :], weights[r][:], inv_sum[:, r : r + 1], 512.0, ALU.mult, ALU.mult)
+            nc.sync.dma_start(out_rows[:, r, :], y[:, r, :])
+
+        row_max(0)
+        exponentiate(0)
+        row_max(1)
+        exponentiate(1)
+        row_max(2)
+        normalise(0, nc.gpsimd)
+        exponentiate(2)
+        row_max(3)
+        normalise(1, nc.gpsimd)
+        exponentiate(3)
+        normalise(2, nc.vector)
+        normalise(3, nc.vector)
+
+        y_bf = sb.tile([P, I, PACK], BF16, name="y_bf", align_bytes=64)
+        y_codes = sb.tile([P, I], U32, name="y_codes", align_bytes=64)
+        y_scales = sb.tile([P, I], U8, name="y_scales", align_bytes=64)
+        y_in = y[:].rearrange("p r (c i) -> p c r i", i=4)
+        y_out = y_bf[:].rearrange("p (c i) r -> p c r i", i=4)
+        nc.vector.tensor_copy(y_out[:, 0 : SPLIT // 4], y_in[:, 0 : SPLIT // 4])
+        nc.scalar.copy(y_out[:, SPLIT // 4 :], y_in[:, SPLIT // 4 :])
+        words = out_1[0].rearrange("p c b -> p (c b)").bitcast(I32)
+        for h in range(2):
+            cols = slice(h * HALF, (h + 1) * HALF)
+            quantize(y_codes[:, cols], y_scales[:, cols], y_bf[:, cols, :].rearrange("p i r -> p (i r)"))
+            nc.sync.dma_start(words[:, cols], y_codes[:, cols].bitcast(I32))
+        for g in range(4):
+            queue = nc.scalar if g % 2 == 0 else nc.sync
+            queue.dma_start(out_2[0, 4 * g : 4 * g + 4, :].bitcast(I32), y_scales[32 * g : 32 * g + 4, :].bitcast(I32))

@@ -20,7 +20,6 @@ AX = mybir.AxisListType
 P = 128
 PACK = 4
 HALF = I // 2
-SPLIT = 320
 
 
 def tile_attend_clippedkeys_pl_kernel(tc, query, keys, dsc, lim, offs, out_0, out_1, out_2):
@@ -83,15 +82,17 @@ def tile_attend_clippedkeys_pl_kernel(tc, query, keys, dsc, lim, offs, out_0, ou
             square_blocks(t, picked, 0, 4)
             for h in range(2):
                 scale_features(t, h, picked[:, h * HALF : (h + 1) * HALF])
-        sum01 = sb.tile([P, 4], F32, name="sum01")
         sum012 = sb.tile([P, 4], F32, name="sum012")
-        nc.gpsimd.tensor_tensor(sum01[:], mean_sq[:, 0, :], mean_sq[:, 1, :], ALU.add)
-        nc.gpsimd.tensor_tensor(sum012[:], sum01[:], mean_sq[:, 2, :], ALU.add)
+        addends = sb.tile([P, 4, PACK - 1], F32, name="addends")
+        for j in range(4):
+            nc.scalar.activation(
+                addends[:, j, :], mean_sq[:, 0 : PACK - 1, j], ACT.Identity, accum_out=sum012[:, j : j + 1]
+            )
 
         last = PACK - 1
         picked_last = [sb.tile([P, HALF], F32, name="picked_last%d" % h) for h in range(2)]
         rms = sb.tile([P, 4], F32, name="rms")
-        inv_rms = sb.tile([P, 4], F32, name="inv_rms")
+        inv_rms = sb.tile([P, 2], F32, name="inv_rms")
         for h in range(2):
             nc.vector.tensor_copy(picked_last[h][:], pool_planes[last][:].indirect(offsets[:, 16 * h : 16 * (h + 1)]))
             square_blocks(last, picked_last[h], 2 * h, 2)
@@ -109,11 +110,11 @@ def tile_attend_clippedkeys_pl_kernel(tc, query, keys, dsc, lim, offs, out_0, ou
         spread = []
         for h in range(2):
             bank = ps.tile([P, I], F32, name="spread%d" % h)
-            nc.vector.reciprocal(inv_rms[:, 2 * h : 2 * h + 2], rms[:, 2 * h : 2 * h + 2])
+            nc.vector.reciprocal(inv_rms[:], rms[:, 2 * h : 2 * h + 2])
             for b in range(2):
                 j = 2 * h + b
                 nc.vector.tensor_scalar(
-                    shrink[:, j : j + 1], inv_rms[:, j : j + 1], lim_cols[:, j : j + 1], 1.0, ALU.mult, ALU.min
+                    shrink[:, j : j + 1], inv_rms[:, b : b + 1], lim_cols[:, j : j + 1], 1.0, ALU.mult, ALU.min
                 )
             for b in range(2):
                 j = 2 * h + b
@@ -128,8 +129,9 @@ def tile_attend_clippedkeys_pl_kernel(tc, query, keys, dsc, lim, offs, out_0, ou
             nc.scalar.copy(q_bf[u][:].rearrange("p e m t -> p m t e"), q_dealt[:, u])
 
         k_bf = [sb.tile([P, HALF, PACK], BF16, name="k_bf%d" % h, align_bytes=64) for h in range(2)]
-        k_codes = [sb.tile([P, HALF], U32, name="k_codes%d" % h, align_bytes=64) for h in range(2)]
-        k_scales = [sb.tile([P, HALF], U8, name="k_scales%d" % h, align_bytes=64) for h in range(2)]
+        k_codes = sb.tile([P, I], U32, name="k_codes", align_bytes=64)
+        k_scales = sb.tile([P, I], U8, name="k_scales", align_bytes=64)
+        halves = [slice(h * HALF, (h + 1) * HALF) for h in range(2)]
 
         def shrink_keys(h):
             nc.vector.tensor_tensor(
@@ -144,37 +146,34 @@ def tile_attend_clippedkeys_pl_kernel(tc, query, keys, dsc, lim, offs, out_0, ou
 
         scores = [ps.tile([P, I], F32, name="scores%d" % r) for r in range(PACK)]
 
-        def score(r, h):
+        def score(r, cols):
             u, e = divmod(r, 2)
             nc.tensor.matmul_mx(
-                out=scores[r][:, h * HALF : (h + 1) * HALF],
+                out=scores[r][:, cols],
                 lhsT=q_codes[u][:, e * P : (e + 1) * P].bitcast(FP8X4),
                 lhsT_scale=q_scales[u][:, e * P : (e + 1) * P],
-                rhs=k_codes[h][:].bitcast(FP8X4),
-                rhs_scale=k_scales[h][:],
+                rhs=k_codes[:, cols].bitcast(FP8X4),
+                rhs_scale=k_scales[:, cols],
                 start=True,
                 stop=True,
             )
 
         def quantize_keys(h):
-            quantize(k_codes[h][:], k_scales[h][:], k_bf[h][:].rearrange("p i t -> p (i t)"))
+            quantize(k_codes[:, halves[h]], k_scales[:, halves[h]], k_bf[h][:].rearrange("p i t -> p (i t)"))
 
         def quantize_queries(u):
             quantize(q_codes[u][:], q_scales[u][:], q_bf[u][:].rearrange("p e m t -> p (e m t)"))
 
         shrink_keys(0)
+        quantize_queries(0)
         shrink_keys(1)
         quantize_keys(0)
-        quantize_queries(0)
-        score(0, 0)
-        score(1, 0)
         quantize_keys(1)
-        score(0, 1)
-        score(1, 1)
         quantize_queries(1)
-        for r in (2, 3):
-            for h in range(2):
-                score(r, h)
+        for h in range(2):
+            score(0, halves[h])
+        for r in range(1, PACK):
+            score(r, slice(0, I))
 
         neg_max = sb.tile([P, PACK], F32, name="neg_max")
         row_sum = sb.tile([P, PACK], F32, name="row_sum")
@@ -191,36 +190,41 @@ def tile_attend_clippedkeys_pl_kernel(tc, query, keys, dsc, lim, offs, out_0, ou
                 weights[r][:], scores[r][:], ACT.Exp, bias=neg_max[:, r : r + 1], accum_out=row_sum[:, r : r + 1]
             )
 
-        def normalise(r, engine):
+        def invert_sum(r):
             nc.vector.reciprocal(inv_sum[:, r : r + 1], row_sum[:, r : r + 1])
-            engine.tensor_scalar(y[:, r, :], weights[r][:], inv_sum[:, r : r + 1], 512.0, ALU.mult, ALU.mult)
+
+        def normalise(r, cols):
+            nc.vector.tensor_scalar(y[:, r, cols], weights[r][:, cols], inv_sum[:, r : r + 1], 512.0, ALU.mult, ALU.mult)
+
+        for r in range(PACK):
+            row_max(r)
+            exponentiate(r)
+        for r in range(PACK - 1):
+            invert_sum(r)
+            normalise(r, slice(0, I))
             nc.sync.dma_start(out_rows[:, r, :], y[:, r, :])
+        invert_sum(last)
+        normalise(last, halves[1])
+        normalise(last, halves[0])
+        nc.sync.dma_start(out_rows[:, last, :], y[:, last, :])
 
-        row_max(0)
-        exponentiate(0)
-        row_max(1)
-        exponentiate(1)
-        row_max(2)
-        normalise(0, nc.gpsimd)
-        exponentiate(2)
-        row_max(3)
-        normalise(1, nc.gpsimd)
-        exponentiate(3)
-        normalise(2, nc.vector)
-        normalise(3, nc.vector)
-
-        y_bf = sb.tile([P, I, PACK], BF16, name="y_bf", align_bytes=64)
+        y_bf = [sb.tile([P, HALF, PACK], BF16, name="y_bf%d" % h, align_bytes=64) for h in range(2)]
         y_codes = sb.tile([P, I], U32, name="y_codes", align_bytes=64)
         y_scales = sb.tile([P, I], U8, name="y_scales", align_bytes=64)
-        y_in = y[:].rearrange("p r (c i) -> p c r i", i=4)
-        y_out = y_bf[:].rearrange("p (c i) r -> p c r i", i=4)
-        nc.vector.tensor_copy(y_out[:, 0 : SPLIT // 4], y_in[:, 0 : SPLIT // 4])
-        nc.scalar.copy(y_out[:, SPLIT // 4 :], y_in[:, SPLIT // 4 :])
+
+        def y_views(h):
+            return (
+                y_bf[h][:].rearrange("p (c i) r -> p c r i", i=4),
+                y[:, :, halves[h]].rearrange("p r (c i) -> p c r i", i=4),
+            )
+
+        nc.scalar.copy(*y_views(1))
+        nc.vector.tensor_copy(*y_views(0))
         words = out_1[0].rearrange("p c b -> p (c b)").bitcast(I32)
         for h in range(2):
-            cols = slice(h * HALF, (h + 1) * HALF)
-            quantize(y_codes[:, cols], y_scales[:, cols], y_bf[:, cols, :].rearrange("p i r -> p (i r)"))
+            cols = halves[h]
+            quantize(y_codes[:, cols], y_scales[:, cols], y_bf[h][:].rearrange("p i r -> p (i r)"))
             nc.sync.dma_start(words[:, cols], y_codes[:, cols].bitcast(I32))
         for g in range(4):
-            queue = nc.scalar if g % 2 == 0 else nc.sync
+            queue = nc.scalar if g < 3 else nc.sync
             queue.dma_start(out_2[0, 4 * g : 4 * g + 4, :].bitcast(I32), y_scales[32 * g : 32 * g + 4, :].bitcast(I32))

@@ -20,6 +20,7 @@ AX = mybir.AxisListType
 P = 128
 PACK = 4
 HALF = I // 2
+SPLIT = 320
 
 
 def tile_attend_clippedkeys_pl_kernel(tc, query, keys, dsc, lim, offs, out_0, out_1, out_2):
@@ -76,12 +77,19 @@ def tile_attend_clippedkeys_pl_kernel(tc, query, keys, dsc, lim, offs, out_0, ou
         def scale_features(t, h, picked):
             nc.vector.tensor_scalar(scaled[h][:, t, :], picked, dsc_cols[:, t : t + 1], None, ALU.mult)
 
+        by_slot = [ps.tile([P, PACK, P], F32, name="by_slot%d" % b, tag="by_slot", bufs=2) for b in range(2)]
+
+        def turn_scaled(t):
+            for b in range(2):
+                nc.tensor.transpose(by_slot[b][:, t, :], scaled[0][:, t, b * P : (b + 1) * P], ident[:])
+
         for t in range(PACK - 1):
             picked = sb.tile([P, I], F32, name="picked%d" % t)
             nc.vector.tensor_copy(picked[:], pool_planes[t][:].indirect(offsets[:]))
             square_blocks(t, picked, 0, 4)
             for h in range(2):
                 scale_features(t, h, picked[:, h * HALF : (h + 1) * HALF])
+            turn_scaled(t)
         sum012 = sb.tile([P, 4], F32, name="sum012")
         addends = sb.tile([P, 4, PACK - 1], F32, name="addends")
         for j in range(4):
@@ -91,7 +99,7 @@ def tile_attend_clippedkeys_pl_kernel(tc, query, keys, dsc, lim, offs, out_0, ou
 
         last = PACK - 1
         picked_last = [sb.tile([P, HALF], F32, name="picked_last%d" % h) for h in range(2)]
-        rms = sb.tile([P, 4], F32, name="rms")
+        rms = sb.tile([P, 4], F32, name="rms", tag="rms", align_bytes=64)
         inv_rms = sb.tile([P, 2], F32, name="inv_rms")
         for h in range(2):
             nc.vector.tensor_copy(picked_last[h][:], pool_planes[last][:].indirect(offsets[:, 16 * h : 16 * (h + 1)]))
@@ -105,46 +113,68 @@ def tile_attend_clippedkeys_pl_kernel(tc, query, keys, dsc, lim, offs, out_0, ou
                 )
         for h in range(2):
             scale_features(last, h, picked_last[h][:])
+        turn_scaled(last)
 
-        shrink = sb.tile([P, 4], F32, name="shrink")
-        spread = []
-        for h in range(2):
-            bank = ps.tile([P, I], F32, name="spread%d" % h)
+        q_bf = [sb.tile([P, 2, P, PACK], BF16, name="q_bf0", align_bytes=64)]
+        q_scales = [sb.tile([P, 2 * P], U8, name="q_scales%d" % u, align_bytes=64) for u in range(2)]
+        q_dealt = q_raw[:].rearrange("p t (m u e) -> p u m t e", u=2, e=2)
+
+        def round_queries(u):
+            nc.vector.tensor_copy(q_bf[u][:].rearrange("p e m t -> p m t e"), q_dealt[:, u])
+
+        shrink = sb.tile([P, 4], F32, name="shrink", tag="shrink", align_bytes=64)
+
+        def shrink_factors(h):
             nc.vector.reciprocal(inv_rms[:], rms[:, 2 * h : 2 * h + 2])
             for b in range(2):
                 j = 2 * h + b
                 nc.vector.tensor_scalar(
                     shrink[:, j : j + 1], inv_rms[:, b : b + 1], lim_cols[:, j : j + 1], 1.0, ALU.mult, ALU.min
                 )
-            for b in range(2):
-                j = 2 * h + b
-                nc.tensor.transpose(bank[:, b * P : (b + 1) * P], shrink[:, j : j + 1].to_broadcast([P, P]), ident[:])
-            spread.append(bank)
 
-        q_bf = [sb.tile([P, 2, P, PACK], BF16, name="q_bf%d" % u, align_bytes=64) for u in range(2)]
-        q_codes = [sb.tile([P, 2 * P], U32, name="q_codes%d" % u, align_bytes=64) for u in range(2)]
-        q_scales = [sb.tile([P, 2 * P], U8, name="q_scales%d" % u, align_bytes=64) for u in range(2)]
-        q_dealt = q_raw[:].rearrange("p t (m u e) -> p u m t e", u=2, e=2)
-        for u in range(2):
-            nc.scalar.copy(q_bf[u][:].rearrange("p e m t -> p m t e"), q_dealt[:, u])
-
-        k_bf = [sb.tile([P, HALF, PACK], BF16, name="k_bf%d" % h, align_bytes=64) for h in range(2)]
+        k_bf = [sb.tile([P, HALF, PACK], BF16, name="k_bf%d" % h, tag="k_bf%d" % h, align_bytes=64) for h in range(2)]
         k_codes = sb.tile([P, I], U32, name="k_codes", align_bytes=64)
         k_scales = sb.tile([P, I], U8, name="k_scales", align_bytes=64)
         halves = [slice(h * HALF, (h + 1) * HALF) for h in range(2)]
 
-        def shrink_keys(h):
-            nc.vector.tensor_tensor(
-                k_bf[h][:].rearrange("p (c i) t -> p c t i", i=4),
-                scaled[h][:].rearrange("p t (c i) -> p c t i", i=4),
-                spread[h][:, 0:HALF].rearrange("p (c i) -> p c i", i=4).unsqueeze(2).to_broadcast([P, HALF // 4, PACK, 4]),
-                ALU.mult,
+        round_queries(0)
+        shrink_factors(0)
+        shrink_factors(1)
+
+        pairs = [sb.tile([P, 2, P, 2], BF16, name="pairs%d" % b) for b in range(2)]
+        for b in range(2):
+            nc.scalar.activation(
+                pairs[b][:],
+                by_slot[b][:].rearrange("i (u e) p -> i u p e", e=2),
+                ACT.Copy,
+                scale=shrink[:, b : b + 1],
             )
+
+        spread = ps.tile([P, I], F32, name="spread")
+        for b in range(2):
+            nc.tensor.transpose(spread[:, b * P : (b + 1) * P], shrink[:, 2 + b : 3 + b].to_broadcast([P, P]), ident[:])
+
+        k_words = k_bf[0][:].rearrange("p i t -> p (i t)").bitcast(F32).rearrange("p (i u) -> p i u", u=2)
+        for b in range(2):
+            back = ps.tile([P, PACK, P], F32, name="back%d" % b)
+            pair_words = pairs[b][:].rearrange("i u p e -> i (u p e)").bitcast(F32)
+            for u in range(2):
+                nc.tensor.transpose(back[:, u, :], pair_words[:, u * P : (u + 1) * P], ident[:])
+            nc.scalar.copy(k_words[:, b * P : (b + 1) * P, :], back[:, 0:2, :].rearrange("p u i -> p i u"))
+
+        q_bf.append(sb.tile([P, 2, P, PACK], BF16, name="q_bf1", tag="rms", align_bytes=64))
+        round_queries(1)
+        nc.vector.tensor_tensor(
+            k_bf[1][:].rearrange("p (c i) t -> p c t i", i=4),
+            scaled[1][:].rearrange("p t (c i) -> p c t i", i=4),
+            spread[:, 0:HALF].rearrange("p (c i) -> p c i", i=4).unsqueeze(2).to_broadcast([P, HALF // 4, PACK, 4]),
+            ALU.mult,
+        )
 
         def quantize(codes, scales, values):
             nc.vector.quantize_mx(out=codes.bitcast(FP8X4), scales=scales, in_=values)
 
-        scores = [ps.tile([P, I], F32, name="scores%d" % r) for r in range(PACK)]
+        scores = [ps.tile([P, I], F32, name="scores%d" % r, tag="turn" if r < 2 else "by_slot", bufs=2) for r in range(PACK)]
 
         def score(r, cols):
             u, e = divmod(r, 2)
@@ -164,13 +194,13 @@ def tile_attend_clippedkeys_pl_kernel(tc, query, keys, dsc, lim, offs, out_0, ou
         def quantize_queries(u):
             quantize(q_codes[u][:], q_scales[u][:], q_bf[u][:].rearrange("p e m t -> p (e m t)"))
 
-        shrink_keys(0)
+        q_codes = [sb.tile([P, 2 * P], U32, name="q_codes0", tag="shrink", align_bytes=64)]
         quantize_queries(0)
-        shrink_keys(1)
-        quantize_keys(0)
         quantize_keys(1)
+        quantize_keys(0)
+        q_codes.append(sb.tile([P, 2 * P], U32, name="q_codes1", tag="k_bf0", align_bytes=64))
         quantize_queries(1)
-        for h in range(2):
+        for h in (1, 0):
             score(0, halves[h])
         for r in range(1, PACK):
             score(r, slice(0, I))
@@ -190,36 +220,47 @@ def tile_attend_clippedkeys_pl_kernel(tc, query, keys, dsc, lim, offs, out_0, ou
                 weights[r][:], scores[r][:], ACT.Exp, bias=neg_max[:, r : r + 1], accum_out=row_sum[:, r : r + 1]
             )
 
-        def invert_sum(r):
-            nc.vector.reciprocal(inv_sum[:, r : r + 1], row_sum[:, r : r + 1])
+        def invert_sums(rows):
+            nc.vector.reciprocal(inv_sum[:, rows], row_sum[:, rows])
 
         def normalise(r, cols):
             nc.vector.tensor_scalar(y[:, r, cols], weights[r][:, cols], inv_sum[:, r : r + 1], 512.0, ALU.mult, ALU.mult)
 
+        def store_rows(r):
+            nc.sync.dma_start(out_rows[:, r, :], y[:, r, :])
+
         for r in range(PACK):
             row_max(r)
             exponentiate(r)
-        for r in range(PACK - 1):
-            invert_sum(r)
-            normalise(r, slice(0, I))
-            nc.sync.dma_start(out_rows[:, r, :], y[:, r, :])
-        invert_sum(last)
-        normalise(last, halves[1])
-        normalise(last, halves[0])
-        nc.sync.dma_start(out_rows[:, last, :], y[:, last, :])
+        factor2 = sb.tile([P, 1], F32, name="factor2")
+        invert_sums(slice(0, 2))
+        invert_sums(slice(2, 3))
+        normalise(0, slice(0, I))
+        store_rows(0)
+        nc.vector.tensor_scalar(factor2[:], inv_sum[:, 2:3], 512.0, None, ALU.mult)
+        normalise(1, slice(0, I))
+        store_rows(1)
+        nc.scalar.activation(y[:, 2, :], weights[2][:], ACT.Copy, scale=factor2[:])
+        store_rows(2)
+        invert_sums(slice(3, 4))
+        normalise(last, slice(SPLIT, I))
+        normalise(last, slice(0, SPLIT))
+        store_rows(last)
 
         y_bf = [sb.tile([P, HALF, PACK], BF16, name="y_bf%d" % h, align_bytes=64) for h in range(2)]
         y_codes = sb.tile([P, I], U32, name="y_codes", align_bytes=64)
         y_scales = sb.tile([P, I], U8, name="y_scales", align_bytes=64)
 
-        def y_views(h):
+        def y_views(first, end):
+            h = first // HALF
             return (
-                y_bf[h][:].rearrange("p (c i) r -> p c r i", i=4),
-                y[:, :, halves[h]].rearrange("p r (c i) -> p c r i", i=4),
+                y_bf[h][:, first - h * HALF : end - h * HALF, :].rearrange("p (c i) r -> p c r i", i=4),
+                y[:, :, first:end].rearrange("p r (c i) -> p c r i", i=4),
             )
 
-        nc.scalar.copy(*y_views(1))
-        nc.vector.tensor_copy(*y_views(0))
+        nc.scalar.copy(*y_views(SPLIT, I))
+        nc.vector.tensor_copy(*y_views(0, HALF))
+        nc.vector.tensor_copy(*y_views(HALF, SPLIT))
         words = out_1[0].rearrange("p c b -> p (c b)").bitcast(I32)
         for h in range(2):
             cols = halves[h]

@@ -31,7 +31,7 @@ def tile_attend_clippedkeys_pl_kernel(tc, query, keys, dsc, lim, offs, out_0, ou
 
         offsets = sb.tile([P, I // 16], U16, name="offsets")
         pool_planes = [sb.tile([P, T], F32, name="pool%d" % t) for t in range(PACK)]
-        q_raw = sb.tile([P, PACK, Q], F32, name="q_raw")
+        q_raw = [sb.tile([P, PACK, Q // 2], F32, name="q_raw%d" % a) for a in range(2)]
         key_rows = keys.rearrange("(p t) n -> p t n", t=PACK)
         nc.sync.dma_start(pool_planes[0][:], key_rows[:, 0, :])
         nc.sync.dma_start(offsets[:], offs)
@@ -42,7 +42,9 @@ def tile_attend_clippedkeys_pl_kernel(tc, query, keys, dsc, lim, offs, out_0, ou
         nc.sync.dma_start(lim_rows[0:4, :], lim.rearrange("(j p) o -> j (p o)", p=P))
         for t in range(1, PACK):
             nc.sync.dma_start(pool_planes[t][:], key_rows[:, t, :])
-        nc.sync.dma_start(q_raw[:], query.rearrange("(p t) n -> p t n", t=PACK))
+        query_rows = query.rearrange("(p t) n -> p t n", t=PACK)
+        for a in range(2):
+            nc.sync.dma_start(q_raw[a][:], query_rows[:, :, a * (Q // 2) : (a + 1) * (Q // 2)])
 
         warm_in = sb.tile([P, 1], F32, name="warm_in")
         warm_out = sb.tile([P, 1], F32, name="warm_out")
@@ -99,8 +101,7 @@ def tile_attend_clippedkeys_pl_kernel(tc, query, keys, dsc, lim, offs, out_0, ou
 
         last = PACK - 1
         picked_last = [sb.tile([P, HALF], F32, name="picked_last%d" % h) for h in range(2)]
-        rms = sb.tile([P, 4], F32, name="rms", tag="rms", align_bytes=64)
-        inv_rms = sb.tile([P, 2], F32, name="inv_rms")
+        rms = sb.tile([P, 4], F32, name="rms")
         for h in range(2):
             nc.vector.tensor_copy(picked_last[h][:], pool_planes[last][:].indirect(offsets[:, 16 * h : 16 * (h + 1)]))
             square_blocks(last, picked_last[h], 2 * h, 2)
@@ -115,21 +116,24 @@ def tile_attend_clippedkeys_pl_kernel(tc, query, keys, dsc, lim, offs, out_0, ou
             scale_features(last, h, picked_last[h][:])
         turn_scaled(last)
 
-        q_bf = [sb.tile([P, 2, P, PACK], BF16, name="q_bf0", align_bytes=64)]
+        q_bf = sb.tile([P, PACK, P, PACK], BF16, name="q_bf", align_bytes=64)
+        inv_rms = q_bf[:, last, P - 2 : P, :].rearrange("p m t -> p (m t)").bitcast(F32)
         q_scales = [sb.tile([P, 2 * P], U8, name="q_scales%d" % u, align_bytes=64) for u in range(2)]
-        q_dealt = q_raw[:].rearrange("p t (m u e) -> p u m t e", u=2, e=2)
 
-        def round_queries(u):
-            nc.vector.tensor_copy(q_bf[u][:].rearrange("p e m t -> p m t e"), q_dealt[:, u])
+        def round_queries(a):
+            nc.vector.tensor_copy(
+                q_bf[:, :, a * (P // 2) : (a + 1) * (P // 2), :].rearrange("p r m t -> p m t r"),
+                q_raw[a][:].rearrange("p t (m r) -> p m t r", r=PACK),
+            )
 
         shrink = sb.tile([P, 4], F32, name="shrink", tag="shrink", align_bytes=64)
 
         def shrink_factors(h):
-            nc.vector.reciprocal(inv_rms[:], rms[:, 2 * h : 2 * h + 2])
+            nc.vector.reciprocal(inv_rms[:, 2 * h : 2 * h + 2], rms[:, 2 * h : 2 * h + 2])
             for b in range(2):
                 j = 2 * h + b
                 nc.vector.tensor_scalar(
-                    shrink[:, j : j + 1], inv_rms[:, b : b + 1], lim_cols[:, j : j + 1], 1.0, ALU.mult, ALU.min
+                    shrink[:, j : j + 1], inv_rms[:, j : j + 1], lim_cols[:, j : j + 1], 1.0, ALU.mult, ALU.min
                 )
 
         k_bf = [sb.tile([P, HALF, PACK], BF16, name="k_bf%d" % h, tag="k_bf%d" % h, align_bytes=64) for h in range(2)]
@@ -162,7 +166,6 @@ def tile_attend_clippedkeys_pl_kernel(tc, query, keys, dsc, lim, offs, out_0, ou
                 nc.tensor.transpose(back[:, u, :], pair_words[:, u * P : (u + 1) * P], ident[:])
             nc.scalar.copy(k_words[:, b * P : (b + 1) * P, :], back[:, 0:2, :].rearrange("p u i -> p i u"))
 
-        q_bf.append(sb.tile([P, 2, P, PACK], BF16, name="q_bf1", tag="rms", align_bytes=64))
         round_queries(1)
         nc.vector.tensor_tensor(
             k_bf[1][:].rearrange("p (c i) t -> p c t i", i=4),
@@ -192,7 +195,7 @@ def tile_attend_clippedkeys_pl_kernel(tc, query, keys, dsc, lim, offs, out_0, ou
             quantize(k_codes[:, halves[h]], k_scales[:, halves[h]], k_bf[h][:].rearrange("p i t -> p (i t)"))
 
         def quantize_queries(u):
-            quantize(q_codes[u][:], q_scales[u][:], q_bf[u][:].rearrange("p e m t -> p (e m t)"))
+            quantize(q_codes[u][:], q_scales[u][:], q_bf[:, 2 * u : 2 * u + 2, :, :].rearrange("p e m t -> p (e m t)"))
 
         q_codes = [sb.tile([P, 2 * P], U32, name="q_codes0", tag="shrink", align_bytes=64)]
         quantize_queries(0)

from contextlib import ExitStack

import concourse.mybir as mybir
from concourse.masks import make_identity

D, T, I, Q = 512, 2048, 512, 512
FLOPS = 2 * D * I * Q

F32 = mybir.dt.float32
BF16 = mybir.dt.bfloat16
I32 = mybir.dt.int32
U32 = mybir.dt.uint32
U16 = mybir.dt.uint16
U8 = mybir.dt.uint8
FP8X4 = mybir.dt.float8_e4m3fn_x4
ALU = mybir.AluOpType
ACT = mybir.ActivationFunctionType
AX = mybir.AxisListType

P = 128
PACK = 4
HALF = I // 2
SPLIT = 320


def tile_attend_clippedkeys_pl_kernel(tc, query, keys, dsc, lim, offs, out_0, out_1, out_2):
    nc = tc.nc
    with ExitStack() as ctx:
        sb = ctx.enter_context(tc.tile_pool(name="sb", bufs=1))
        ps = ctx.enter_context(tc.psum_pool(name="ps", bufs=1))

        offsets = sb.tile([P, I // 16], U16, name="offsets")
        pool_planes = [sb.tile([P, T], F32, name="pool%d" % t) for t in range(PACK)]
        q_raw = [sb.tile([P, PACK, Q // 2], F32, name="q_raw%d" % a) for a in range(2)]
        key_rows = keys.rearrange("(p t) n -> p t n", t=PACK)
        nc.sync.dma_start(pool_planes[0][:], key_rows[:, 0, :])
        nc.sync.dma_start(offsets[:], offs)
        dsc_cols = sb.tile([P, PACK], F32, name="dsc_cols")
        nc.sync.dma_start(dsc_cols[:], dsc.rearrange("o (p t) -> p (o t)", t=PACK))
        lim_rows = sb.tile([P, P], F32, name="lim_rows")
        nc.gpsimd.memset(lim_rows[:], 0.0)
        nc.sync.dma_start(lim_rows[0:4, :], lim.rearrange("(j p) o -> j (p o)", p=P))
        for t in range(1, PACK):
            nc.sync.dma_start(pool_planes[t][:], key_rows[:, t, :])
        query_rows = query.rearrange("(p t) n -> p t n", t=PACK)
        for a in range(2):
            nc.sync.dma_start(q_raw[a][:], query_rows[:, :, a * (Q // 2) : (a + 1) * (Q // 2)])

        warm_in = sb.tile([P, 1], F32, name="warm_in")
        warm_out = sb.tile([P, 1], F32, name="warm_out")
        nc.vector.memset(warm_in[:], 1.0)
        nc.scalar.activation(warm_out[:], warm_in[:], ACT.Sqrt)

        ident = sb.tile([P, P], F32, name="ident")
        make_identity(nc, ident[:])
        lim_ps = ps.tile([P, I], F32, name="lim_ps", tag="turn", bufs=2)
        nc.tensor.transpose(lim_ps[:, 0:P], lim_rows[:], ident[:])
        lim_cols = sb.tile([P, 4], F32, name="lim_cols")
        nc.scalar.copy(lim_cols[:], lim_ps[:, 0:4])

        squares = sb.tile([P, PACK, I], BF16, name="squares")
        mean_sq = sb.tile([P, PACK, 4], F32, name="mean_sq")
        scaled = [sb.tile([P, PACK, HALF], F32, name="scaled%d" % h) for h in range(2)]

        def square_blocks(t, picked, first_block, n_blocks):
            turned = ps.tile([P, I], F32, name="turned", tag="turn", bufs=2)
            for b in range(n_blocks):
                nc.tensor.transpose(turned[:, b * P : (b + 1) * P], picked[:, b * P : (b + 1) * P], ident[:])
            for b in range(n_blocks):
                j = first_block + b
                nc.scalar.activation(
                    squares[:, t, j * P : (j + 1) * P],
                    turned[:, b * P : (b + 1) * P],
                    ACT.Square,
                    scale=D**-0.5,
                    accum_out=mean_sq[:, t, j : j + 1],
                )

        def scale_features(t, h, picked):
            nc.vector.tensor_scalar(scaled[h][:, t, :], picked, dsc_cols[:, t : t + 1], None, ALU.mult)

        by_slot = [ps.tile([P, PACK, P], F32, name="by_slot%d" % b, tag="by_slot", bufs=2) for b in range(2)]

        def turn_scaled(t):
            for b in range(2):
                nc.tensor.transpose(by_slot[b][:, t, :], scaled[0][:, t, b * P : (b + 1) * P], ident[:])

        for t in range(PACK - 1):
            picked = sb.tile([P, I], F32, name="picked%d" % t)
            nc.vector.tensor_copy(picked[:], pool_planes[t][:].indirect(offsets[:]))
            square_blocks(t, picked, 0, 4)
            for h in range(2):
                scale_features(t, h, picked[:, h * HALF : (h + 1) * HALF])
            turn_scaled(t)
        sum012 = sb.tile([P, 4], F32, name="sum012")
        addends = sb.tile([P, 4, PACK - 1], F32, name="addends")
        for j in range(4):
            nc.scalar.activation(
                addends[:, j, :], mean_sq[:, 0 : PACK - 1, j], ACT.Identity, accum_out=sum012[:, j : j + 1]
            )

        last = PACK - 1
        picked_last = [sb.tile([P, HALF], F32, name="picked_last%d" % h) for h in range(2)]
        rms = sb.tile([P, 4], F32, name="rms")
        for h in range(2):
            nc.vector.tensor_copy(picked_last[h][:], pool_planes[last][:].indirect(offsets[:, 16 * h : 16 * (h + 1)]))
            square_blocks(last, picked_last[h], 2 * h, 2)
            for j in (2 * h, 2 * h + 1):
                nc.scalar.activation(
                    rms[:, j : j + 1],
                    mean_sq[:, last, j : j + 1],
                    ACT.Sqrt,
                    bias=sum012[:, j : j + 1],
                )
        for h in range(2):
            scale_features(last, h, picked_last[h][:])
        turn_scaled(last)

        q_bf = sb.tile([P, PACK, P, PACK], BF16, name="q_bf", align_bytes=64)
        inv_rms = q_bf[:, last, P - 2 : P, :].rearrange("p m t -> p (m t)").bitcast(F32)
        q_scales = [sb.tile([P, 2 * P], U8, name="q_scales%d" % u, align_bytes=64) for u in range(2)]

        def round_queries(a):
            nc.vector.tensor_copy(
                q_bf[:, :, a * (P // 2) : (a + 1) * (P // 2), :].rearrange("p r m t -> p m t r"),
                q_raw[a][:].rearrange("p t (m r) -> p m t r", r=PACK),
            )

        shrink = sb.tile([P, 4], F32, name="shrink", tag="shrink", align_bytes=64)

        def shrink_factors(h):
            nc.vector.reciprocal(inv_rms[:, 2 * h : 2 * h + 2], rms[:, 2 * h : 2 * h + 2])
            for b in range(2):
                j = 2 * h + b
                nc.vector.tensor_scalar(
                    shrink[:, j : j + 1], inv_rms[:, j : j + 1], lim_cols[:, j : j + 1], 1.0, ALU.mult, ALU.min
                )

        k_bf = [sb.tile([P, HALF, PACK], BF16, name="k_bf%d" % h, tag="k_bf%d" % h, align_bytes=64) for h in range(2)]
        k_codes = sb.tile([P, I], U32, name="k_codes", align_bytes=64)
        k_scales = sb.tile([P, I], U8, name="k_scales", align_bytes=64)
        halves = [slice(h * HALF, (h + 1) * HALF) for h in range(2)]

        round_queries(0)
        shrink_factors(0)
        shrink_factors(1)

        pairs = [sb.tile([P, 2, P, 2], BF16, name="pairs%d" % b) for b in range(2)]
        for b in range(2):
            nc.scalar.activation(
                pairs[b][:],
                by_slot[b][:].rearrange("i (u e) p -> i u p e", e=2),
                ACT.Copy,
                scale=shrink[:, b : b + 1],
            )

        spread = ps.tile([P, I], F32, name="spread")
        for b in range(2):
            nc.tensor.transpose(spread[:, b * P : (b + 1) * P], shrink[:, 2 + b : 3 + b].to_broadcast([P, P]), ident[:])

        k_words = k_bf[0][:].rearrange("p i t -> p (i t)").bitcast(F32).rearrange("p (i u) -> p i u", u=2)
        for b in range(2):
            back = ps.tile([P, PACK, P], F32, name="back%d" % b)
            pair_words = pairs[b][:].rearrange("i u p e -> i (u p e)").bitcast(F32)
            for u in range(2):
                nc.tensor.transpose(back[:, u, :], pair_words[:, u * P : (u + 1) * P], ident[:])
            nc.scalar.copy(k_words[:, b * P : (b + 1) * P, :], back[:, 0:2, :].rearrange("p u i -> p i u"))

        round_queries(1)
        nc.vector.tensor_tensor(
            k_bf[1][:].rearrange("p (c i) t -> p c t i", i=4),
            scaled[1][:].rearrange("p t (c i) -> p c t i", i=4),
            spread[:, 0:HALF].rearrange("p (c i) -> p c i", i=4).unsqueeze(2).to_broadcast([P, HALF // 4, PACK, 4]),
            ALU.mult,
        )

        def quantize(codes, scales, values):
            nc.vector.quantize_mx(out=codes.bitcast(FP8X4), scales=scales, in_=values)

        scores = [ps.tile([P, I], F32, name="scores%d" % r, tag="turn" if r < 2 else "by_slot", bufs=2) for r in range(PACK)]

        def score(r, cols):
            u, e = divmod(r, 2)
            nc.tensor.matmul_mx(
                out=scores[r][:, cols],
                lhsT=q_codes[u][:, e * P : (e + 1) * P].bitcast(FP8X4),
                lhsT_scale=q_scales[u][:, e * P : (e + 1) * P],
                rhs=k_codes[:, cols].bitcast(FP8X4),
                rhs_scale=k_scales[:, cols],
                start=True,
                stop=True,
            )

        def quantize_keys(h):
            quantize(k_codes[:, halves[h]], k_scales[:, halves[h]], k_bf[h][:].rearrange("p i t -> p (i t)"))

        def quantize_queries(u):
            quantize(q_codes[u][:], q_scales[u][:], q_bf[:, 2 * u : 2 * u + 2, :, :].rearrange("p e m t -> p (e m t)"))

        q_codes = [sb.tile([P, 2 * P], U32, name="q_codes0", tag="shrink", align_bytes=64)]
        quantize_queries(0)
        quantize_keys(1)
        quantize_keys(0)
        q_codes.append(sb.tile([P, 2 * P], U32, name="q_codes1", tag="k_bf0", align_bytes=64))
        quantize_queries(1)
        for h in (1, 0):
            score(0, halves[h])
        for r in range(1, PACK):
            score(r, slice(0, I))

        neg_max = sb.tile([P, PACK], F32, name="neg_max")
        row_sum = sb.tile([P, PACK], F32, name="row_sum")
        inv_sum = sb.tile([P, PACK], F32, name="inv_sum")
        weights = [sb.tile([P, I], F32, name="weights%d" % r) for r in range(PACK)]
        y = sb.tile([P, PACK, I], F32, name="y")
        out_rows = out_0.rearrange("(p r) i -> p r i", r=PACK)

        def row_max(r):
            nc.vector.tensor_reduce(neg_max[:, r : r + 1], scores[r][:], AX.X, ALU.max, negate=True)

        def exponentiate(r):
            nc.scalar.activation(
                weights[r][:], scores[r][:], ACT.Exp, bias=neg_max[:, r : r + 1], accum_out=row_sum[:, r : r + 1]
            )

        def invert_sums(rows):
            nc.vector.reciprocal(inv_sum[:, rows], row_sum[:, rows])

        def normalise(r, cols):
            nc.vector.tensor_scalar(y[:, r, cols], weights[r][:, cols], inv_sum[:, r : r + 1], 512.0, ALU.mult, ALU.mult)

        def store_rows(r):
            nc.sync.dma_start(out_rows[:, r, :], y[:, r, :])

        for r in range(PACK):
            row_max(r)
            exponentiate(r)
        factor2 = sb.tile([P, 1], F32, name="factor2")
        invert_sums(slice(0, 2))
        invert_sums(slice(2, 3))
        normalise(0, slice(0, I))
        store_rows(0)
        nc.vector.tensor_scalar(factor2[:], inv_sum[:, 2:3], 512.0, None, ALU.mult)
        normalise(1, slice(0, I))
        store_rows(1)
        nc.scalar.activation(y[:, 2, :], weights[2][:], ACT.Copy, scale=factor2[:])
        store_rows(2)
        invert_sums(slice(3, 4))
        normalise(last, slice(SPLIT, I))
        normalise(last, slice(0, SPLIT))
        store_rows(last)

        y_bf = [sb.tile([P, HALF, PACK], BF16, name="y_bf%d" % h, align_bytes=64) for h in range(2)]
        y_codes = sb.tile([P, I], U32, name="y_codes", align_bytes=64)
        y_scales = sb.tile([P, I], U8, name="y_scales", align_bytes=64)

        def y_views(first, end):
            h = first // HALF
            return (
                y_bf[h][:, first - h * HALF : end - h * HALF, :].rearrange("p (c i) r -> p c r i", i=4),
                y[:, :, first:end].rearrange("p r (c i) -> p c r i", i=4),
            )

        nc.scalar.copy(*y_views(SPLIT, I))
        nc.vector.tensor_copy(*y_views(0, HALF))
        nc.vector.tensor_copy(*y_views(HALF, SPLIT))
        words = out_1[0].rearrange("p c b -> p (c b)").bitcast(I32)
        for h in range(2):
            cols = halves[h]
            quantize(y_codes[:, cols], y_scales[:, cols], y_bf[h][:].rearrange("p i r -> p (i r)"))
            nc.sync.dma_start(words[:, cols], y_codes[:, cols].bitcast(I32))
        for g in range(4):
            queue = nc.scalar if g < 3 else nc.sync
            queue.dma_start(out_2[0, 4 * g : 4 * g + 4, :].bitcast(I32), y_scales[32 * g : 32 * g + 4, :].bitcast(I32))
